import numpy as np
import ml_dtypes


def mxq(x, axis, fmt="e4m3"):
    dtype, down = {"e4m3": (ml_dtypes.float8_e4m3fn, 7), "e5m2": (ml_dtypes.float8_e5m2, 14)}[fmt]
    v = np.moveaxis(np.asarray(x, np.float32).astype(ml_dtypes.bfloat16).astype(np.float64), axis, -1)
    blocks = v.reshape(v.shape[:-1] + (-1, 32))
    amax = np.abs(blocks).max(-1, keepdims=True)
    byte = np.maximum(np.where(amax > 0, np.frexp(amax)[1] - 1 + 127, 0) - down, 1)
    scale = np.exp2(byte - 127.0)
    codes = (blocks / scale).astype(np.float32).astype(dtype).astype(np.float64)
    return np.moveaxis((codes * scale).reshape(v.shape), -1, axis)


WIDE = False


def mx_kscale(k):
    if not WIDE:
        return np.ones(k)
    levels = np.array([10, -10, 5, -5, 0])
    if k % 512:
        return np.exp2(np.random.permutation(np.resize(levels, k // 32))).repeat(32)
    a = np.empty((k // 512, 16))
    for p in range(k // 512):
        a[p, :8] = np.random.permutation(np.resize(levels, 8))
        for g in range(8):
            far = levels[np.abs(levels - a[p, g]) >= 10]
            a[p, g + 8] = far[np.random.randint(len(far))]
    return np.exp2(a.ravel()).repeat(32)


def f64(x):
    return np.asarray(x).astype(np.float64)


def striped(idx):
    return np.tile(idx.reshape(-1, 16).T, (8, 1)).astype(np.uint16)


def unstriped(offs):
    return offs[:16].T.reshape(-1).astype(np.int64)


E2M1 = np.array([0.0, 0.5, 1.0, 1.5, 2.0, 3.0, 4.0, 6.0, -0.0, -0.5, -1.0, -1.5, -2.0, -3.0, -4.0, -6.0])


def pack_weight(w, fmt):
    k, n = w.shape
    w = f64(np.asarray(w, np.float32).astype(ml_dtypes.bfloat16)).reshape(k // 32, 32, n)
    amax = np.abs(w).max(1)
    if fmt == "e4m3":
        byte = np.frexp(amax)[1] - 1 + 127 - 7
    else:
        mant, ex = np.frexp(amax / 6.0)
        byte = np.where(mant > 0.5, ex, ex - 1) + 127
    byte = np.clip(np.where(amax > 0, byte, 1), 1, 254)
    scaled = (w * np.exp2(127.0 - byte)[:, None, :]).reshape(k, n).astype(np.float32)
    by_word = np.ascontiguousarray(scaled.reshape(k // 512, 128, 4, n).transpose(0, 1, 3, 2))
    if fmt == "e4m3":
        words = by_word.astype(ml_dtypes.float8_e4m3fn).view(np.uint8)
    else:
        c = by_word.astype(ml_dtypes.float4_e2m1fn).view(np.uint8) & 0xF
        words = (c[..., 0::2] | (c[..., 1::2] << 4)).reshape(k // 512, 128, 2 * n)
    return np.ascontiguousarray(words), np.ascontiguousarray(byte.astype(np.uint8).reshape(k // 512, 16, n))


def unpack_weight(words, scales, fmt):
    g, _, n = scales.shape
    words = np.ascontiguousarray(words).reshape(g, 128, n, -1)
    if fmt == "e4m3":
        vals = words.view(ml_dtypes.float8_e4m3fn).astype(np.float64)
    else:
        nib = np.empty((g, 128, n, 4), np.uint8)
        nib[..., 0::2] = words & 0xF
        nib[..., 1::2] = words >> 4
        vals = E2M1[nib]
    vals = vals * np.repeat(np.exp2(scales.astype(np.float64) - 127.0), 8, axis=1)[..., None]
    return vals.transpose(0, 1, 3, 2).reshape(g * 512, n)


def gelu(v):
    return 0.5 * v * (1.0 + np.tanh(np.sqrt(2.0 / np.pi) * (v + 0.044715 * v**3)))


def often(T, S):
    return np.random.permutation(T)[(T * np.random.uniform(0, 1, S) ** 4).astype(np.int64)]


K, K2, H, N, T, S, P = 1024, 512, 1024, 512, 4096, 1024, 512


def setup_inputs():
    n = np.random.standard_normal
    s, s2, u = mx_kscale(K)[:, None], mx_kscale(K2)[:, None], mx_kscale(H)[:, None]
    d = {}
    d["tab_words"], d["tab_scales"] = pack_weight(n((K, T)) * s, "e4m3")
    d["tab2_words"], d["tab2_scales"] = pack_weight(n((K2, T)) * s2, "e4m3")
    d["tab3_words"], d["tab3_scales"] = pack_weight(n((K2, T)) * s2, "e4m3")
    d["offs"] = striped(np.random.permutation(T)[:S])
    d["offs2"] = striped(np.random.permutation(T)[:S])
    d["offs3"] = striped(np.random.permutation(T)[:S])
    d["pos1"] = striped(np.random.permutation(S)[:P])
    d["pos2"] = striped(often(S, P))
    d["pos3"] = striped(often(S, P))
    d["w1"] = (n((K, H)) / K**0.5 / s * u.T).astype(np.float32)
    d["w2_words"], d["w2_scales"] = pack_weight(n((K2, H)) / K2**0.5 / s2 * u.T, "e4m3")
    d["w3"] = (n((K2, H)) / K2**0.5 / s2 * u.T).astype(np.float32)
    d["w4_words"], d["w4_scales"] = pack_weight(n((H, N)) / H**0.5 / u, "e2m1")
    d["w5"] = (0.25 * n((H, N)) / H**0.5 / u).astype(np.float32)
    return d


def reference(tab_words, tab_scales, tab2_words, tab2_scales, tab3_words, tab3_scales,
              offs, offs2, offs3, pos1, pos2, pos3,
              w1, w2_words, w2_scales, w3, w4_words, w4_scales, w5):
    v = unpack_weight(tab_words, tab_scales, "e4m3")[:, unstriped(offs)]
    v2 = unpack_weight(tab2_words, tab2_scales, "e4m3")[:, unstriped(offs2)]
    v3 = unpack_weight(tab3_words, tab3_scales, "e4m3")[:, unstriped(offs3)]
    a = mxq(f64(w1), 0, "e4m3").T @ v
    b = unpack_weight(w2_words, w2_scales, "e4m3").T @ v2
    d = mxq(f64(w3), 0, "e4m3").T @ v3
    bp = b[:, unstriped(pos2)]
    z = np.abs(a[:, unstriped(pos1)] - bp) + np.abs(bp - d[:, unstriped(pos3)])
    zq = mxq(z, 0, "e4m3")
    e = unpack_weight(w4_words, w4_scales, "e2m1").T @ zq
    y = mxq(f64(w5), 0, "e4m3").T @ zq
    return 1.0 / (1.0 + np.exp(-e)) + y

@@ -1,0 +1,341 @@
+from contextlib import ExitStack
+
+import concourse.mybir as mybir
+from concourse.masks import make_identity
+
+K, K2, H, N, T, S, J = 1024, 512, 1024, 512, 4096, 1024, 512
+FLOPS = 2 * H * S * (K + 2 * K2) + 2 * 2 * H * N * J
+
+F32 = mybir.dt.float32
+BF16 = mybir.dt.bfloat16
+I32 = mybir.dt.int32
+U32 = mybir.dt.uint32
+U16 = mybir.dt.uint16
+U8 = mybir.dt.uint8
+FP8X4 = mybir.dt.float8_e4m3fn_x4
+FP4X4 = mybir.dt.float4_e2m1fn_x4
+ACT = mybir.ActivationFunctionType
+ALU = mybir.AluOpType
+
+P = 128
+PACK = 4
+KP = P * PACK
+BANK = 512
+KIB = 1024
+B_WINDOWS = 3
+BANKS = 8
+WORK = 80
+
+
+def tile_list_driving_test_assignment_kernel(
+    tc, tab_words, tab_scales, tab2_words, tab2_scales, tab3_words, tab3_scales,
+    offs, offs2, offs3, pos1, pos2, pos3,
+    w1, w2_words, w2_scales, w3, w4_words, w4_scales, w5, out,
+):
+    nc = tc.nc
+    with ExitStack() as ctx:
+        lists = ctx.enter_context(tc.tile_pool(name="lists", bufs=1))
+        keep = ctx.enter_context(tc.tile_pool(name="keep", bufs=1))
+        arena = ctx.enter_context(tc.tile_pool(name="arena", bufs=1))
+        ring = ctx.enter_context(tc.tile_pool(name="ring", bufs=1))
+        psum = ctx.enter_context(tc.psum_pool(name="psum", bufs=1))
+
+        banks_taken = []
+        last_bank = {}
+        ring_of = {"turn": range(BANKS), "product": range(BANKS)}
+
+        def next_bank(kind):
+            banks = ring_of[kind]
+            n = last_bank.get(banks, -1) + 1
+            last_bank[banks] = n
+            bank = psum.tile([P, BANK], F32, name="bank%d" % len(banks_taken), offset=banks[n % len(banks)] * 2 * KIB)
+            banks_taken.append(bank)
+            return bank
+
+        def load_list(source, name):
+            tile = lists.tile(list(source.shape), U16, name=name)
+            nc.sync.dma_start(tile[:], source)
+            return tile
+
+        def placed(shape, dtype, name, kib):
+            return arena.tile(shape, dtype, name=name, offset=kib * KIB, align_bytes=64)
+
+        def zeroed_plane(tile):
+            nc.vector.memset(tile[:].bitcast(I32), 0)
+            return tile
+
+        def load_table_scales(window, scales, first_row):
+            passes = scales.shape[0]
+            for q in range(4):
+                rows = slice(32 * q + first_row, 32 * q + first_row + 4 * passes)
+                source = scales[:, 4 * q : 4 * q + 4, :] if passes > 1 else scales[0, 4 * q : 4 * q + 4, :]
+                nc.sync.dma_start(window[rows, :].bitcast(I32), source.bitcast(I32))
+
+        def load_words(tile, words):
+            nc.sync.dma_start(tile[:], words.rearrange("p t i -> p (t i)").bitcast(I32))
+
+        def gather_scales(window, offsets, name):
+            picked = keep.tile([P, S], U8, name=name, align_bytes=64)
+            nc.vector.tensor_copy(picked[:], window[:].indirect(offsets[:]))
+            return picked
+
+        def gather_words(window, offsets, name):
+            halves = []
+            for h in range(2):
+                picked = keep.tile([P, BANK], U32, name="%s_%d" % (name, h), align_bytes=64)
+                nc.vector.tensor_copy(picked[:], window[:].bitcast(U32).indirect(offsets[:, 32 * h : 32 * (h + 1)]))
+                halves.append(picked)
+            return halves
+
+        def load_weight(rows):
+            raw = ring.tile([P, PACK, BANK], F32, name="raw", bufs=3)
+            nc.sync.dma_start(raw[:], rows.rearrange("(p t) c -> p t c", t=PACK))
+            return raw
+
+        def quantize_weight(raw, name, on_scalar, slot):
+            rounded = placed([P, PACK * BANK], BF16, name + "_rounded", WORK + 4 * slot)
+            dst = rounded[:].rearrange("p (c i t) -> p c t i", i=4, t=PACK)
+            src = raw[:].rearrange("p t (c i) -> p c t i", i=4)
+            if on_scalar:
+                nc.scalar.copy(dst, src)
+            else:
+                nc.vector.tensor_copy(dst, src)
+            codes = keep.tile([P, BANK], U32, name=name + "_codes", align_bytes=64)
+            plane = keep.tile([P, BANK], U8, name=name + "_plane", align_bytes=64)
+            nc.vector.quantize_mx(out=codes[:].bitcast(FP8X4), scales=plane[:], in_=rounded[:])
+            return codes, plane
+
+        def first_stage(window, passes):
+            for h in range(2):
+                bank = next_bank("product")
+                for i, (codes, plane, halves, picked_plane, row) in enumerate(passes):
+                    nc.tensor.matmul_mx(
+                        out=bank[:], lhsT=codes.bitcast(FP8X4), lhsT_scale=plane,
+                        rhs=halves[h][:].bitcast(FP8X4),
+                        rhs_scale=picked_plane[row:P, BANK * h : BANK * (h + 1)],
+                        start=(i == 0), stop=(i == len(passes) - 1),
+                    )
+                nc.scalar.copy(window[:, BANK * h : BANK * (h + 1)], bank[:])
+
+        def add_transposed(bank, first, second):
+            terms = first + second
+            for i, (c, x) in enumerate(terms):
+                nc.tensor.matmul(
+                    bank[:, P * c : P * (c + 1)], lhsT=x, rhs=ident[:],
+                    start=(i == 0), stop=(i == len(terms) - 1), is_transpose=True,
+                )
+
+        def abs_difference(result, minus_b, picked):
+            bank = next_bank("turn")
+            add_transposed(bank, list(enumerate(picked))[::-1], list(enumerate(minus_b)))
+            nc.scalar.activation(
+                out=result[:].rearrange("j (t m) -> j t m", t=PACK),
+                in_=bank[:].rearrange("j (m t) -> j t m", t=PACK), func=ACT.Abs,
+            )
+
+        sc2_win = zeroed_plane(placed([P, T], U8, "sc2_win", 48))
+        sc3_win = zeroed_plane(placed([P, T], U8, "sc3_win", 52))
+        sc1_win = zeroed_plane(placed([P, T], U8, "sc1_win", 56))
+        w2_plane = zeroed_plane(keep.tile([P, H], U8, name="w2_plane", align_bytes=64))
+        w4_plane = zeroed_plane(keep.tile([P, 2 * N], U8, name="w4_plane", align_bytes=64))
+        b_win = [keep.tile([P, 2 * S], F32, name="b_win%d" % i) for i in range(B_WINDOWS)]
+        ident = keep.tile([P, P], F32, name="ident")
+        for window in b_win:
+            nc.gpsimd.memset(window[:, S:], 0.0)
+        make_identity(nc, ident[:])
+
+        idx2 = load_list(offs2, "idx2")
+        idx3 = load_list(offs3, "idx3")
+        idx1 = load_list(offs, "idx1")
+        p2 = load_list(pos2, "p2")
+        p3 = load_list(pos3, "p3")
+        p1 = load_list(pos1, "p1")
+        w3_raw0 = ring.tile([P, PACK, BANK], F32, name="raw", bufs=3)
+        for h in range(2):
+            cols = slice(256 * h, 256 * (h + 1))
+            nc.sync.dma_start(w3_raw0[:, :, cols], w3[:, cols].rearrange("(p t) c -> p t c", t=PACK))
+        load_table_scales(sc2_win, tab2_scales, 8)
+        load_table_scales(sc3_win, tab3_scales, 12)
+        tab2_win = placed([P, T], I32, "tab2_win", 0)
+        load_words(tab2_win, tab2_words[0])
+        load_table_scales(w2_plane, w2_scales, 0)
+        w2_codes = keep.tile([P, H], I32, name="w2_codes", align_bytes=64)
+        load_words(w2_codes, w2_words[0])
+        tab3_win = placed([P, T], I32, "tab3_win", 16)
+        load_words(tab3_win, tab3_words[0])
+        w3_raw1 = load_weight(w3[:, BANK : 2 * BANK])
+        tab_win = [placed([P, T], I32, "tab_win0", 32), placed([P, T], I32, "tab_win1", 0)]
+
+        sc2 = gather_scales(sc2_win, idx2, "sc2")
+        sc3 = gather_scales(sc3_win, idx3, "sc3")
+        w3_q0 = quantize_weight(w3_raw0, "w3_0", True, 0)
+        v2 = gather_words(tab2_win, idx2, "v2")
+        v3 = gather_words(tab3_win, idx3, "v3")
+        load_words(tab_win[0], tab_words[0])
+        load_table_scales(sc1_win, tab_scales, 0)
+        load_words(tab_win[1], tab_words[1])
+
+        minus_b = []
+
+        def make_minus_b(s):
+            window = b_win[s % B_WINDOWS]
+            cols = slice(P * s, P * (s + 1))
+            first_stage(window, [(w2_codes[:, cols], w2_plane[:, cols], v2, sc2, 8)])
+            picked = keep.tile([P, J], F32, name="minus_b%d" % s)
+            nc.vector.tensor_scalar(picked[:], window[:].indirect(p2[:]), -1.0, 0.0, ALU.mult, ALU.add)
+            minus_b.append(picked)
+
+        dist_bd = {}
+        v1 = []
+
+        def make_d(g, weight):
+            codes, plane = weight
+            windows = []
+            for i in range(4):
+                window = placed([P, S], F32, "d_win%d%d" % (g, i), 64 - 16 * g + 4 * i)
+                cols = slice(P * i, P * (i + 1))
+                first_stage(window, [(codes[:, cols], plane[:, cols], v3, sc3, 12)])
+                windows.append(window)
+            return windows
+
+        def make_a_slice(g, i, weights):
+            window = placed([P, S], F32, "a_win%d%d" % (g, i), 32 * (1 - g) + 4 * i)
+            cols = slice(P * i, P * (i + 1))
+            first_stage(window, [(weights[a][0][:, cols], weights[a][1][:, cols], v1[a], sc1, 4 * a) for a in range(2)])
+            return window
+
+        def make_a(g, weights):
+            return [make_a_slice(g, i, weights) for i in range(4)]
+
+        def pick(windows, offsets, name, places):
+            picked = []
+            entries = 16 * offsets.shape[1]
+            for i, window in enumerate(windows):
+                tile = placed([P, entries], F32, "%s%d" % (name, i), WORK + places[i])
+                nc.vector.tensor_copy(tile[:], window[:].indirect(offsets))
+                picked.append(tile)
+            return picked
+
+        def make_dist_bd(g, blocks, picked):
+            for i, jb in enumerate(blocks):
+                result = placed([P, KP], F32, "dist_bd%d%d" % (g, jb), 16 + 2 * (4 * g + jb))
+                abs_difference(
+                    result,
+                    [minus_b[4 * g + s][:, P * jb : P * (jb + 1)] for s in range(4)],
+                    [x[:, P * i : P * (i + 1)] for x in picked],
+                )
+                dist_bd[g, jb] = result
+
+        def w1_part(a, g, on_scalar, slot):
+            raw = load_weight(w1[KP * a : KP * (a + 1), BANK * g : BANK * (g + 1)])
+            return quantize_weight(raw, "w1_%d%d" % (a, g), on_scalar, slot)
+
+        z_q = {}
+
+        def make_dist_ab(g, jb, picked):
+            cols = slice(P * jb, P * (jb + 1))
+            dist_ab = ring.tile([P, KP], F32, name="dist_ab", bufs=3)
+            abs_difference(dist_ab, [minus_b[4 * g + i][:, cols] for i in range(4)], picked)
+            return dist_ab
+
+        def make_z(g, jb, dist_ab):
+            bank = next_bank("turn")
+            add_transposed(
+                bank,
+                [(t, dist_ab[:, P * t : P * (t + 1)]) for t in range(PACK)],
+                [(t, dist_bd[g, jb][:, P * t : P * (t + 1)]) for t in range(PACK)],
+            )
+            rounded = placed([P, KP], BF16, "z_rounded%d%d" % (g, jb), WORK + 4 * (4 + g) + jb)
+            nc.scalar.copy(
+                rounded[:].rearrange("p (j t) -> p j t", t=PACK),
+                bank[:].rearrange("p (t j) -> p j t", t=PACK),
+            )
+            codes = keep.tile([P, P], U32, name="z_codes%d%d" % (g, jb), align_bytes=64)
+            plane = keep.tile([P, P], U8, name="z_plane%d%d" % (g, jb), align_bytes=64)
+            nc.vector.quantize_mx(out=codes[:].bitcast(FP8X4), scales=plane[:], in_=rounded[:])
+            z_q[g, jb] = (codes, plane)
+
+        def second_stage(jb):
+            e_bank = next_bank("product")
+            y_bank = next_bank("product")
+            for nb in range(4):
+                cols = slice(P * nb, P * (nb + 1))
+                for g in range(2):
+                    first = 2 * N * g + 2 * P * nb
+                    nc.tensor.matmul_mx(
+                        out=e_bank[:, cols], lhsT=w4_codes[:, first : first + 2 * P].bitcast(FP4X4),
+                        lhsT_scale=w4_plane[:, N * g + P * nb : N * g + P * (nb + 1)],
+                        rhs=z_q[g, jb][0][:].bitcast(FP8X4), rhs_scale=z_q[g, jb][1][:],
+                        start=(g == 0), stop=(g == 1),
+                    )
+            for nb in range(4):
+                cols = slice(P * nb, P * (nb + 1))
+                for g in range(2):
+                    nc.tensor.matmul_mx(
+                        out=y_bank[:, cols], lhsT=w5_q[g][0][:, cols].bitcast(FP8X4), lhsT_scale=w5_q[g][1][:, cols],
+                        rhs=z_q[g, jb][0][:].bitcast(FP8X4), rhs_scale=z_q[g, jb][1][:],
+                        start=(g == 0), stop=(g == 1),
+                    )
+            gate = ring.tile([P, BANK], F32, name="gate", bufs=2)
+            nc.scalar.activation(out=gate[:], in_=e_bank[:], func=ACT.Sigmoid)
+            result = ring.tile([P, BANK], F32, name="result", bufs=2)
+            nc.vector.tensor_tensor(result[:], y_bank[:], gate[:], ALU.add)
+            nc.sync.dma_start(
+                out.rearrange("(nb p) j -> p nb j", p=P)[:, :, P * jb : P * (jb + 1)],
+                result[:].rearrange("p (nb j) -> p nb j", nb=4),
+            )
+
+        w3_q1 = quantize_weight(w3_raw1, "w3_1", True, 1)
+        for s in range(6):
+            make_minus_b(s)
+        d_win0 = make_d(0, w3_q0)
+        for s in range(6, 8):
+            make_minus_b(s)
+        d_win1 = make_d(1, w3_q1)
+        v1.append(gather_words(tab_win[0], idx1, "v1_0"))
+        sc1 = gather_scales(sc1_win, idx1, "sc1")
+        v1.append(gather_words(tab_win[1], idx1, "v1_1"))
+        w1_q0 = [w1_part(a, 0, True, 4 + a) for a in range(2)]
+        make_dist_bd(0, range(4), pick(d_win0, p3[:], "d_picked0", [8, 10, 12, 14]))
+        a_win0 = make_a(0, w1_q0)
+        w1_q1 = [w1_part(a, 1, False, 4 + a) for a in range(2)]
+        a_win1 = make_a(1, w1_q1)
+        picked = pick(a_win0, p1[:], "a_picked0", [8, 10, 12, 14])
+        dist = [make_dist_ab(0, jb, [x[:, P * jb : P * (jb + 1)] for x in picked]) for jb in range(2)]
+        for jb in range(4):
+            if jb + 2 < 4:
+                dist.append(make_dist_ab(0, jb + 2, [x[:, P * (jb + 2) : P * (jb + 3)] for x in picked]))
+            make_z(0, jb, dist[jb])
+        w5_q = []
+        for g in range(2):
+            raw = load_weight(w5[KP * g : KP * (g + 1), :])
+            w5_q.append(quantize_weight(raw, "w5_%d" % g, False, g))
+        w4_codes = keep.tile([P, 2 * 2 * N], U8, name="w4_codes", align_bytes=64)
+        nc.sync.dma_start(
+            w4_codes[:].bitcast(I32).rearrange("p (a c) -> p a c", a=2),
+            w4_words.bitcast(I32).rearrange("a p c -> p a c"),
+        )
+        for q in range(4):
+            nc.sync.dma_start(
+                w4_plane[32 * q : 32 * q + 4, :].bitcast(I32).rearrange("r (a c) -> r a c", a=2),
+                w4_scales[:, 4 * q : 4 * q + 4, :].bitcast(I32).rearrange("a r c -> r a c"),
+            )
+
+        def blocks_of(picked):
+            return [[x[:, P * i : P * (i + 1)] for x in picked] for i in range(2)]
+
+        ring_of["turn"], ring_of["product"] = range(0, 4), range(4, 8)
+        make_dist_bd(1, (0, 1), pick(d_win1, p3[:, 0:16], "d_picked10", [0, 1, 2, 3]))
+        picked = blocks_of(pick(a_win1, p1[:, 0:16], "a_picked10", [4, 5, 6, 7]))
+        dist = [make_dist_ab(1, jb, picked[jb]) for jb in range(2)]
+        for jb in range(2):
+            make_z(1, jb, dist[jb])
+        make_dist_bd(1, (2, 3), pick(d_win1, p3[:, 16:32], "d_picked11", [16, 17, 18, 19]))
+        picked = blocks_of(pick(a_win1, p1[:, 16:32], "a_picked11", [0, 1, 20, 21]))
+        second_stage(0)
+        dist = [make_dist_ab(1, 2 + i, picked[i]) for i in range(2)]
+        second_stage(1)
+        for i in range(2):
+            make_z(1, 2 + i, dist[i])
+        for jb in range(2, 4):
+            second_stage(jb)

@@ -25,6 +25,7 @@ KIB = 1024
 B_WINDOWS = 3
 BANKS = 8
 WORK = 80
+DEALT = [False, True]
 
 
 def tile_list_driving_test_assignment_kernel(
@@ -52,6 +53,8 @@ def tile_list_driving_test_assignment_kernel(
             banks_taken.append(bank)
             return bank
 
+        raws = []
+
         def load_list(source, name):
             tile = lists.tile(list(source.shape), U16, name=name)
             nc.sync.dma_start(tile[:], source)
@@ -64,12 +67,12 @@ def tile_list_driving_test_assignment_kernel(
             nc.vector.memset(tile[:].bitcast(I32), 0)
             return tile
 
-        def load_table_scales(window, scales, first_row):
+        def load_table_scales(window, scales, first_row, queue):
             passes = scales.shape[0]
             for q in range(4):
                 rows = slice(32 * q + first_row, 32 * q + first_row + 4 * passes)
                 source = scales[:, 4 * q : 4 * q + 4, :] if passes > 1 else scales[0, 4 * q : 4 * q + 4, :]
-                nc.sync.dma_start(window[rows, :].bitcast(I32), source.bitcast(I32))
+                queue.dma_start(window[rows, :].bitcast(I32), source.bitcast(I32))
 
         def load_words(tile, words):
             nc.sync.dma_start(tile[:], words.rearrange("p t i -> p (t i)").bitcast(I32))
@@ -88,14 +91,18 @@ def tile_list_driving_test_assignment_kernel(
             return halves
 
         def load_weight(rows):
-            raw = ring.tile([P, PACK, BANK], F32, name="raw", bufs=3)
+            raw = placed([P, PACK, BANK], F32, "raw%d" % len(raws), 128 + 8 * (len(raws) % 4))
+            raws.append(raw)
             nc.sync.dma_start(raw[:], rows.rearrange("(p t) c -> p t c", t=PACK))
             return raw
 
-        def quantize_weight(raw, name, on_scalar, slot):
+        def quantize_weight(raw, name, on_scalar, slot, dealt=False):
             rounded = placed([P, PACK * BANK], BF16, name + "_rounded", WORK + 4 * slot)
             dst = rounded[:].rearrange("p (c i t) -> p c t i", i=4, t=PACK)
             src = raw[:].rearrange("p t (c i) -> p c t i", i=4)
+            if dealt:
+                dst = rounded[:].rearrange("p (u m t) -> p m u t", u=PACK, t=PACK)
+                src = raw[:].rearrange("p t (m u) -> p m u t", u=PACK)
             if on_scalar:
                 nc.scalar.copy(dst, src)
             else:
@@ -133,15 +140,27 @@ def tile_list_driving_test_assignment_kernel(
                 in_=bank[:].rearrange("j (m t) -> j t m", t=PACK), func=ACT.Abs,
             )
 
+        def w2_part(g):
+            cols = slice(KP * g, KP * (g + 1))
+            if not DEALT[g]:
+                return w2_codes[:, cols], w2_plane[:, cols]
+            codes = keep.tile([P, KP], I32, name="w2_dealt_codes%d" % g, align_bytes=64)
+            plane = keep.tile([P, KP], U8, name="w2_dealt_plane%d" % g, align_bytes=64)
+            for dst, src in ((codes, w2_codes), (plane, w2_plane)):
+                nc.vector.tensor_copy(
+                    dst[:].rearrange("p (u m) -> p m u", u=PACK), src[:, cols].rearrange("p (m u) -> p m u", u=PACK)
+                )
+            return codes[:], plane[:]
+
         sc2_win = zeroed_plane(placed([P, T], U8, "sc2_win", 48))
         sc3_win = zeroed_plane(placed([P, T], U8, "sc3_win", 52))
-        sc1_win = zeroed_plane(placed([P, T], U8, "sc1_win", 56))
         w2_plane = zeroed_plane(keep.tile([P, H], U8, name="w2_plane", align_bytes=64))
+        sc1_win = zeroed_plane(placed([P, T], U8, "sc1_win", 56))
         w4_plane = zeroed_plane(keep.tile([P, 2 * N], U8, name="w4_plane", align_bytes=64))
-        b_win = [keep.tile([P, 2 * S], F32, name="b_win%d" % i) for i in range(B_WINDOWS)]
+        b_win = [placed([P, 2 * S], F32, "b_win%d" % i, 104 + 8 * i) for i in range(B_WINDOWS)]
         ident = keep.tile([P, P], F32, name="ident")
         for window in b_win:
-            nc.gpsimd.memset(window[:, S:], 0.0)
+            nc.vector.memset(window[:, S:], 0.0)
         make_identity(nc, ident[:])
 
         idx2 = load_list(offs2, "idx2")
@@ -150,39 +169,42 @@ def tile_list_driving_test_assignment_kernel(
         p2 = load_list(pos2, "p2")
         p3 = load_list(pos3, "p3")
         p1 = load_list(pos1, "p1")
-        w3_raw0 = ring.tile([P, PACK, BANK], F32, name="raw", bufs=3)
-        for h in range(2):
-            cols = slice(256 * h, 256 * (h + 1))
-            nc.sync.dma_start(w3_raw0[:, :, cols], w3[:, cols].rearrange("(p t) c -> p t c", t=PACK))
-        load_table_scales(sc2_win, tab2_scales, 8)
-        load_table_scales(sc3_win, tab3_scales, 12)
+        w3_raw0 = load_weight(w3[:, 0:BANK])
+        w1_raw00 = load_weight(w1[0:KP, 0:BANK])
+        load_table_scales(sc2_win, tab2_scales, 8, nc.sync)
         tab2_win = placed([P, T], I32, "tab2_win", 0)
         load_words(tab2_win, tab2_words[0])
-        load_table_scales(w2_plane, w2_scales, 0)
         w2_codes = keep.tile([P, H], I32, name="w2_codes", align_bytes=64)
         load_words(w2_codes, w2_words[0])
+        load_table_scales(w2_plane, w2_scales, 0, nc.sync)
         tab3_win = placed([P, T], I32, "tab3_win", 16)
         load_words(tab3_win, tab3_words[0])
-        w3_raw1 = load_weight(w3[:, BANK : 2 * BANK])
+        load_table_scales(sc3_win, tab3_scales, 12, nc.sync)
         tab_win = [placed([P, T], I32, "tab_win0", 32), placed([P, T], I32, "tab_win1", 0)]
+        load_words(tab_win[0], tab_words[0])
+        load_table_scales(sc1_win, tab_scales, 0, nc.sync)
 
         sc2 = gather_scales(sc2_win, idx2, "sc2")
-        sc3 = gather_scales(sc3_win, idx3, "sc3")
-        w3_q0 = quantize_weight(w3_raw0, "w3_0", True, 0)
+        w3_q0 = quantize_weight(w3_raw0, "w3_0", True, 0, DEALT[0])
+        w1_q0 = [quantize_weight(w1_raw00, "w1_00", True, 1, DEALT[0])]
         v2 = gather_words(tab2_win, idx2, "v2")
-        v3 = gather_words(tab3_win, idx3, "v3")
-        load_words(tab_win[0], tab_words[0])
-        load_table_scales(sc1_win, tab_scales, 0)
+        w2_q = [w2_part(0), w2_part(1)]
         load_words(tab_win[1], tab_words[1])
 
         minus_b = []
 
-        def make_minus_b(s):
-            window = b_win[s % B_WINDOWS]
-            cols = slice(P * s, P * (s + 1))
-            first_stage(window, [(w2_codes[:, cols], w2_plane[:, cols], v2, sc2, 8)])
-            picked = keep.tile([P, J], F32, name="minus_b%d" % s)
-            nc.vector.tensor_scalar(picked[:], window[:].indirect(p2[:]), -1.0, 0.0, ALU.mult, ALU.add)
+        def make_b(s):
+            cols = slice(P * (s % 4), P * (s % 4 + 1))
+            picked = placed([P, J], F32, "b_picked%d" % s, [160, 162, 52, 54, 24, 26, 28, 30][s])
+            passes = [(w2_q[s // 4][0][:, cols], w2_q[s // 4][1][:, cols], v2, sc2, 8)]
+            if s < 4:
+                window = b_win[s % B_WINDOWS]
+                first_stage(window, passes)
+                nc.vector.tensor_scalar(picked[:], window[:].indirect(p2[:]), -1.0, 0.0, ALU.mult, ALU.add)
+            else:
+                window = placed([P, S], F32, "b_win%d" % s, [48, 60, 168, 172][s - 4])
+                first_stage(window, passes)
+                nc.vector.tensor_copy(picked[:], window[:].indirect(p2[:]))
             minus_b.append(picked)
 
         dist_bd = {}
@@ -192,14 +214,14 @@ def tile_list_driving_test_assignment_kernel(
             codes, plane = weight
             windows = []
             for i in range(4):
-                window = placed([P, S], F32, "d_win%d%d" % (g, i), 64 - 16 * g + 4 * i)
+                window = placed([P, S], F32, "d_win%d%d" % (g, i), [[64, 68, 72, 76], [48, 56, 60, 164]][g][i])
                 cols = slice(P * i, P * (i + 1))
                 first_stage(window, [(codes[:, cols], plane[:, cols], v3, sc3, 12)])
                 windows.append(window)
             return windows
 
         def make_a_slice(g, i, weights):
-            window = placed([P, S], F32, "a_win%d%d" % (g, i), 32 * (1 - g) + 4 * i)
+            window = placed([P, S], F32, "a_win%d%d" % (g, i), [[32, 36, 40, 44], [0, 4, 8, 12]][g][i])
             cols = slice(P * i, P * (i + 1))
             first_stage(window, [(weights[a][0][:, cols], weights[a][1][:, cols], v1[a], sc1, 4 * a) for a in range(2)])
             return window
@@ -228,7 +250,7 @@ def tile_list_driving_test_assignment_kernel(
 
         def w1_part(a, g, on_scalar, slot):
             raw = load_weight(w1[KP * a : KP * (a + 1), BANK * g : BANK * (g + 1)])
-            return quantize_weight(raw, "w1_%d%d" % (a, g), on_scalar, slot)
+            return quantize_weight(raw, "w1_%d%d" % (a, g), on_scalar, slot, DEALT[g])
 
         z_q = {}
 
@@ -246,70 +268,83 @@ def tile_list_driving_test_assignment_kernel(
                 [(t, dist_bd[g, jb][:, P * t : P * (t + 1)]) for t in range(PACK)],
             )
             rounded = placed([P, KP], BF16, "z_rounded%d%d" % (g, jb), WORK + 4 * (4 + g) + jb)
-            nc.scalar.copy(
+            copy = nc.vector.tensor_copy if jb >= 2 else nc.scalar.copy
+            copy(
                 rounded[:].rearrange("p (j t) -> p j t", t=PACK),
                 bank[:].rearrange("p (t j) -> p j t", t=PACK),
             )
             codes = keep.tile([P, P], U32, name="z_codes%d%d" % (g, jb), align_bytes=64)
             plane = keep.tile([P, P], U8, name="z_plane%d%d" % (g, jb), align_bytes=64)
             nc.vector.quantize_mx(out=codes[:].bitcast(FP8X4), scales=plane[:], in_=rounded[:])
-            z_q[g, jb] = (codes, plane)
+            z_q[g, jb] = (codes[:], plane[:])
 
-        def second_stage(jb):
-            e_bank = next_bank("product")
-            y_bank = next_bank("product")
-            for nb in range(4):
-                cols = slice(P * nb, P * (nb + 1))
-                for g in range(2):
-                    first = 2 * N * g + 2 * P * nb
+        def second_pass(jb, g, banks):
+            for bank, codes, plane, width, dtype in (
+                (banks[0], w4_codes[:, 2 * N * g : 2 * N * (g + 1)], w4_plane[:, N * g : N * (g + 1)], 2 * P, FP4X4),
+                (banks[1], w5_q[g][0][:], w5_q[g][1][:], P, FP8X4),
+            ):
+                for nb in range(4):
                     nc.tensor.matmul_mx(
-                        out=e_bank[:, cols], lhsT=w4_codes[:, first : first + 2 * P].bitcast(FP4X4),
-                        lhsT_scale=w4_plane[:, N * g + P * nb : N * g + P * (nb + 1)],
-                        rhs=z_q[g, jb][0][:].bitcast(FP8X4), rhs_scale=z_q[g, jb][1][:],
-                        start=(g == 0), stop=(g == 1),
+                        out=bank[:, P * nb : P * (nb + 1)],
+                        lhsT=codes[:, width * nb : width * (nb + 1)].bitcast(dtype),
+                        lhsT_scale=plane[:, P * nb : P * (nb + 1)],
+                        rhs=z_q[g, jb][0].bitcast(FP8X4), rhs_scale=z_q[g, jb][1],
+                        start=(g == 0 and nb == 0), stop=(g == 1 and nb == 3),
                     )
-            for nb in range(4):
-                cols = slice(P * nb, P * (nb + 1))
-                for g in range(2):
-                    nc.tensor.matmul_mx(
-                        out=y_bank[:, cols], lhsT=w5_q[g][0][:, cols].bitcast(FP8X4), lhsT_scale=w5_q[g][1][:, cols],
-                        rhs=z_q[g, jb][0][:].bitcast(FP8X4), rhs_scale=z_q[g, jb][1][:],
-                        start=(g == 0), stop=(g == 1),
-                    )
-            gate = ring.tile([P, BANK], F32, name="gate", bufs=2)
-            nc.scalar.activation(out=gate[:], in_=e_bank[:], func=ACT.Sigmoid)
-            result = ring.tile([P, BANK], F32, name="result", bufs=2)
-            nc.vector.tensor_tensor(result[:], y_bank[:], gate[:], ALU.add)
+
+        def finish(jb, banks):
+            gate = placed([P, BANK], F32, "gate%d" % jb, 64 + 4 * jb)
+            nc.scalar.activation(out=gate[:], in_=banks[0][:], func=ACT.Sigmoid)
+            result = placed([P, BANK], F32, "result%d" % jb, 66 + 4 * jb)
+            nc.vector.tensor_tensor(result[:], banks[1][:], gate[:], ALU.add)
             nc.sync.dma_start(
                 out.rearrange("(nb p) j -> p nb j", p=P)[:, :, P * jb : P * (jb + 1)],
                 result[:].rearrange("p (nb j) -> p nb j", nb=4),
             )
 
-        w3_q1 = quantize_weight(w3_raw1, "w3_1", True, 1)
-        for s in range(6):
-            make_minus_b(s)
+        def distance(windows, offsets, g, first, count, name, place, result):
+            diff = placed([P, PACK, count], F32, name, place)
+            for u in range(PACK):
+                nc.vector.tensor_tensor(
+                    diff[:, u, :], windows[u][:].indirect(offsets[:, first // 16 : (first + count) // 16]),
+                    minus_b[4 * g + u][:, first : first + count], ALU.subtract,
+                )
+            return diff
+
+        def absolute(diff, result, first, count):
+            nc.scalar.activation(
+                out=result.rearrange("p (c i u) -> p c u i", i=4, u=PACK),
+                in_=diff[:, :, first : first + count].rearrange("p u (c i) -> p c u i", i=4), func=ACT.Abs,
+            )
+
+        def join(g, jb0, blocks, x, y, place):
+            rounded = placed([P, KP * blocks], BF16, "z_rounded%d%d" % (g, jb0), place)
+            nc.vector.tensor_tensor(rounded[:], x, y, ALU.add)
+            codes = keep.tile([P, P * blocks], U32, name="z_codes%d%d" % (g, jb0), align_bytes=64)
+            plane = keep.tile([P, P * blocks], U8, name="z_plane%d%d" % (g, jb0), align_bytes=64)
+            nc.vector.quantize_mx(out=codes[:].bitcast(FP8X4), scales=plane[:], in_=rounded[:])
+            for i in range(blocks):
+                z_q[g, jb0 + i] = (codes[:, P * i : P * (i + 1)], plane[:, P * i : P * (i + 1)])
+
+        for s in range(4):
+            make_b(s)
+        v3 = gather_words(tab3_win, idx3, "v3")
+        sc3 = gather_scales(sc3_win, idx3, "sc3")
+        for s in range(4, 8):
+            make_b(s)
         d_win0 = make_d(0, w3_q0)
-        for s in range(6, 8):
-            make_minus_b(s)
-        d_win1 = make_d(1, w3_q1)
         v1.append(gather_words(tab_win[0], idx1, "v1_0"))
         sc1 = gather_scales(sc1_win, idx1, "sc1")
         v1.append(gather_words(tab_win[1], idx1, "v1_1"))
-        w1_q0 = [w1_part(a, 0, True, 4 + a) for a in range(2)]
-        make_dist_bd(0, range(4), pick(d_win0, p3[:], "d_picked0", [8, 10, 12, 14]))
+        w3_q1 = quantize_weight(load_weight(w3[:, BANK : 2 * BANK]), "w3_1", True, 0, DEALT[1])
+        w1_q1 = [w1_part(0, 1, True, 1), w1_part(1, 1, True, 5)]
+        w1_q0.append(w1_part(1, 0, True, 4))
+        w5_q = [quantize_weight(load_weight(w5[0:KP, :]), "w5_0", True, 2)]
         a_win0 = make_a(0, w1_q0)
-        w1_q1 = [w1_part(a, 1, False, 4 + a) for a in range(2)]
-        a_win1 = make_a(1, w1_q1)
+        d_win1 = make_d(1, w3_q1)
+        make_dist_bd(0, range(4), pick(d_win0, p3[:], "d_picked0", [136 - WORK, 138 - WORK, 140 - WORK, 142 - WORK]))
         picked = pick(a_win0, p1[:], "a_picked0", [8, 10, 12, 14])
-        dist = [make_dist_ab(0, jb, [x[:, P * jb : P * (jb + 1)] for x in picked]) for jb in range(2)]
-        for jb in range(4):
-            if jb + 2 < 4:
-                dist.append(make_dist_ab(0, jb + 2, [x[:, P * (jb + 2) : P * (jb + 3)] for x in picked]))
-            make_z(0, jb, dist[jb])
-        w5_q = []
-        for g in range(2):
-            raw = load_weight(w5[KP * g : KP * (g + 1), :])
-            w5_q.append(quantize_weight(raw, "w5_%d" % g, False, g))
+        w5_q.append(quantize_weight(load_weight(w5[KP : 2 * KP, :]), "w5_1", True, 4))
         w4_codes = keep.tile([P, 2 * 2 * N], U8, name="w4_codes", align_bytes=64)
         nc.sync.dma_start(
             w4_codes[:].bitcast(I32).rearrange("p (a c) -> p a c", a=2),
@@ -321,21 +356,24 @@ def tile_list_driving_test_assignment_kernel(
                 w4_scales[:, 4 * q : 4 * q + 4, :].bitcast(I32).rearrange("a r c -> r a c"),
             )
 
-        def blocks_of(picked):
-            return [[x[:, P * i : P * (i + 1)] for x in picked] for i in range(2)]
-
-        ring_of["turn"], ring_of["product"] = range(0, 4), range(4, 8)
-        make_dist_bd(1, (0, 1), pick(d_win1, p3[:, 0:16], "d_picked10", [0, 1, 2, 3]))
-        picked = blocks_of(pick(a_win1, p1[:, 0:16], "a_picked10", [4, 5, 6, 7]))
-        dist = [make_dist_ab(1, jb, picked[jb]) for jb in range(2)]
-        for jb in range(2):
-            make_z(1, jb, dist[jb])
-        make_dist_bd(1, (2, 3), pick(d_win1, p3[:, 16:32], "d_picked11", [16, 17, 18, 19]))
-        picked = blocks_of(pick(a_win1, p1[:, 16:32], "a_picked11", [0, 1, 20, 21]))
-        second_stage(0)
-        dist = [make_dist_ab(1, 2 + i, picked[i]) for i in range(2)]
-        second_stage(1)
-        for i in range(2):
-            make_z(1, 2 + i, dist[i])
-        for jb in range(2, 4):
-            second_stage(jb)
+        diff_d = distance(d_win1, p3, 1, 0, J, "diff_d", WORK, None)
+        a_win1 = make_a(1, w1_q1)
+        dist = [make_dist_ab(0, jb, [x[:, P * jb : P * (jb + 1)] for x in picked]) for jb in range(2)]
+        for jb in range(4):
+            if jb + 2 < 4:
+                dist.append(make_dist_ab(0, jb + 2, [x[:, P * (jb + 2) : P * (jb + 3)] for x in picked]))
+            make_z(0, jb, dist[jb])
+        banks = [(next_bank("product"), next_bank("product")) for jb in range(4)]
+        for jb in range(4):
+            second_pass(jb, 0, banks[jb])
+        dist_d = placed([P, 4 * J], F32, "dist_d", 16)
+        for half in range(2):
+            absolute(diff_d, dist_d[:, 1024 * half : 1024 * (half + 1)], 256 * half, 256)
+            diff = distance(a_win1, p1, 1, 256 * half, 256, "diff_a%d" % half, [WORK + 20, 48][half], None)
+            for i in range(2):
+                jb = 2 * half + i
+                dist_a = ring.tile([P, KP], F32, name="dist_ab", bufs=3)
+                absolute(diff, dist_a[:], P * i, P)
+                join(1, jb, 1, dist_a[:], dist_d[:, KP * jb : KP * (jb + 1)], WORK + 8 + jb)
+                second_pass(jb, 1, banks[jb])
+                finish(jb, banks[jb])

@@ -67,12 +67,24 @@ def tile_list_driving_test_assignment_kernel(
             nc.vector.memset(tile[:].bitcast(I32), 0)
             return tile
 
-        def load_table_scales(window, scales, first_row, queue):
-            passes = scales.shape[0]
+        def load_plane(plane, scales):
             for q in range(4):
-                rows = slice(32 * q + first_row, 32 * q + first_row + 4 * passes)
-                source = scales[:, 4 * q : 4 * q + 4, :] if passes > 1 else scales[0, 4 * q : 4 * q + 4, :]
-                queue.dma_start(window[rows, :].bitcast(I32), source.bitcast(I32))
+                nc.sync.dma_start(plane[32 * q : 32 * q + 4, :].bitcast(I32), scales[0, 4 * q : 4 * q + 4, :].bitcast(I32))
+
+        def load_spread(window, scales):
+            passes = scales.shape[0]
+            source = scales.bitcast(I32).rearrange("a i t -> i a t") if passes > 1 else scales[0].bitcast(I32)
+            nc.sync.dma_start(window[0 : P : 8 // passes, :].bitcast(I32), source)
+
+        def gather_plane(window, offsets, passes, plane, name):
+            picked = gather_scales(window, offsets, name)
+            for a in range(passes):
+                for q in range(4):
+                    first = 32 * q + 4 * a
+                    nc.gpsimd.dma_start(
+                        plane[first : first + 4, :].bitcast(I32), picked[first : 32 * (q + 1) : 8, :].bitcast(I32)
+                    )
+            return plane
 
         def load_words(tile, words):
             nc.sync.dma_start(tile[:], words.rearrange("p t i -> p (t i)").bitcast(I32))
@@ -82,33 +94,37 @@ def tile_list_driving_test_assignment_kernel(
             nc.vector.tensor_copy(picked[:], window[:].indirect(offsets[:]))
             return picked
 
-        def gather_words(window, offsets, name):
+        def gather_words(window, offsets, name, place):
             halves = []
             for h in range(2):
-                picked = keep.tile([P, BANK], U32, name="%s_%d" % (name, h), align_bytes=64)
+                picked = placed([P, BANK], U32, "%s_%d" % (name, h), place + 2 * h)
                 nc.vector.tensor_copy(picked[:], window[:].bitcast(U32).indirect(offsets[:, 32 * h : 32 * (h + 1)]))
                 halves.append(picked)
             return halves
 
-        def load_weight(rows):
-            raw = placed([P, PACK, BANK], F32, "raw%d" % len(raws), 128 + 8 * (len(raws) % 4))
+        def load_weight(rows, kib):
+            raw = placed([P, PACK, rows.shape[1]], F32, "raw%d" % len(raws), kib)
             raws.append(raw)
             nc.sync.dma_start(raw[:], rows.rearrange("(p t) c -> p t c", t=PACK))
             return raw
 
-        def quantize_weight(raw, name, on_scalar, slot, dealt=False):
-            rounded = placed([P, PACK * BANK], BF16, name + "_rounded", WORK + 4 * slot)
+        def quantize_weight(raw, name, on_scalar, place, dealt=False, kept=None):
+            rounded = placed([P, PACK * BANK], BF16, name + "_rounded", place)
             dst = rounded[:].rearrange("p (c i t) -> p c t i", i=4, t=PACK)
-            src = raw[:].rearrange("p t (c i) -> p c t i", i=4)
+            src = raw.rearrange("p t (c i) -> p c t i", i=4)
             if dealt:
                 dst = rounded[:].rearrange("p (u m t) -> p m u t", u=PACK, t=PACK)
-                src = raw[:].rearrange("p t (m u) -> p m u t", u=PACK)
+                src = raw.rearrange("p t (m u) -> p m u t", u=PACK)
             if on_scalar:
                 nc.scalar.copy(dst, src)
             else:
                 nc.vector.tensor_copy(dst, src)
-            codes = keep.tile([P, BANK], U32, name=name + "_codes", align_bytes=64)
-            plane = keep.tile([P, BANK], U8, name=name + "_plane", align_bytes=64)
+            if kept is None:
+                codes = keep.tile([P, BANK], U32, name=name + "_codes", align_bytes=64)
+                plane = keep.tile([P, BANK], U8, name=name + "_plane", align_bytes=64)
+            else:
+                codes = placed([P, BANK], U32, name + "_codes", kept[0])
+                plane = placed([P, BANK], U8, name + "_plane", kept[1])
             nc.vector.quantize_mx(out=codes[:].bitcast(FP8X4), scales=plane[:], in_=rounded[:])
             return codes, plane
 
@@ -153,10 +169,12 @@ def tile_list_driving_test_assignment_kernel(
             return codes[:], plane[:]
 
         sc2_win = zeroed_plane(placed([P, T], U8, "sc2_win", 48))
-        sc3_win = zeroed_plane(placed([P, T], U8, "sc3_win", 52))
-        w2_plane = zeroed_plane(keep.tile([P, H], U8, name="w2_plane", align_bytes=64))
+        sc3_win = placed([P, T], U8, "sc3_win", 52)
+        nc.gpsimd.memset(sc3_win[:].bitcast(I32), 0)
         sc1_win = zeroed_plane(placed([P, T], U8, "sc1_win", 56))
+        w2_plane = zeroed_plane(keep.tile([P, H], U8, name="w2_plane", align_bytes=64))
         w4_plane = zeroed_plane(keep.tile([P, 2 * N], U8, name="w4_plane", align_bytes=64))
+        planes = [zeroed_plane(placed([P, S], U8, "plane%d" % i, kib)) for i, kib in enumerate((180, WORK, 181))]
         b_win = [placed([P, 2 * S], F32, "b_win%d" % i, 104 + 8 * i) for i in range(B_WINDOWS)]
         ident = keep.tile([P, P], F32, name="ident")
         for window in b_win:
@@ -166,28 +184,30 @@ def tile_list_driving_test_assignment_kernel(
         idx2 = load_list(offs2, "idx2")
         idx3 = load_list(offs3, "idx3")
         idx1 = load_list(offs, "idx1")
+        w3_raw = [load_weight(w3[:, 0:BANK], 128)]
         p2 = load_list(pos2, "p2")
         p3 = load_list(pos3, "p3")
         p1 = load_list(pos1, "p1")
-        w3_raw0 = load_weight(w3[:, 0:BANK])
-        w1_raw00 = load_weight(w1[0:KP, 0:BANK])
-        load_table_scales(sc2_win, tab2_scales, 8, nc.sync)
-        tab2_win = placed([P, T], I32, "tab2_win", 0)
+        load_spread(sc2_win, tab2_scales)
+        load_spread(sc3_win, tab3_scales)
+        load_spread(sc1_win, tab_scales)
+        w3_raw.append(load_weight(w3[:, BANK : 2 * BANK], 136))
+        tab2_win = placed([P, T], I32, "tab2_win", 184)
         load_words(tab2_win, tab2_words[0])
         w2_codes = keep.tile([P, H], I32, name="w2_codes", align_bytes=64)
         load_words(w2_codes, w2_words[0])
-        load_table_scales(w2_plane, w2_scales, 0, nc.sync)
+        load_plane(w2_plane, w2_scales)
         tab3_win = placed([P, T], I32, "tab3_win", 16)
         load_words(tab3_win, tab3_words[0])
-        load_table_scales(sc3_win, tab3_scales, 12, nc.sync)
         tab_win = [placed([P, T], I32, "tab_win0", 32), placed([P, T], I32, "tab_win1", 0)]
         load_words(tab_win[0], tab_words[0])
-        load_table_scales(sc1_win, tab_scales, 0, nc.sync)
 
-        sc2 = gather_scales(sc2_win, idx2, "sc2")
-        w3_q0 = quantize_weight(w3_raw0, "w3_0", True, 0, DEALT[0])
-        w1_q0 = [quantize_weight(w1_raw00, "w1_00", True, 1, DEALT[0])]
-        v2 = gather_words(tab2_win, idx2, "v2")
+        sc2 = gather_plane(sc2_win, idx2, 1, planes[0], "sc2")
+        sc3 = gather_plane(sc3_win, idx3, 1, planes[1], "sc3")
+        w3_q = [quantize_weight(w3_raw[0][:], "w3_0", True, WORK + 8, DEALT[0])]
+        sc1 = gather_plane(sc1_win, idx1, 2, planes[2], "sc1")
+        w3_q.append(quantize_weight(w3_raw[1][:], "w3_1", True, WORK + 12, DEALT[1], (WORK + 4, WORK + 20)))
+        v2 = gather_words(tab2_win, idx2, "v2", 176)
         w2_q = [w2_part(0), w2_part(1)]
         load_words(tab_win[1], tab_words[1])
 
@@ -195,14 +215,14 @@ def tile_list_driving_test_assignment_kernel(
 
         def make_b(s):
             cols = slice(P * (s % 4), P * (s % 4 + 1))
-            picked = placed([P, J], F32, "b_picked%d" % s, [160, 162, 52, 54, 24, 26, 28, 30][s])
-            passes = [(w2_q[s // 4][0][:, cols], w2_q[s // 4][1][:, cols], v2, sc2, 8)]
+            picked = placed([P, J], F32, "b_picked%d" % s, [160, 162, 16, 18, 24, 26, 28, 30][s])
+            passes = [(w2_q[s // 4][0][:, cols], w2_q[s // 4][1][:, cols], v2, sc2, 0)]
             if s < 4:
                 window = b_win[s % B_WINDOWS]
                 first_stage(window, passes)
                 nc.vector.tensor_scalar(picked[:], window[:].indirect(p2[:]), -1.0, 0.0, ALU.mult, ALU.add)
             else:
-                window = placed([P, S], F32, "b_win%d" % s, [48, 60, 168, 172][s - 4])
+                window = placed([P, S], F32, "b_win%d" % s, [48, 52, 168, 172][s - 4])
                 first_stage(window, passes)
                 nc.vector.tensor_copy(picked[:], window[:].indirect(p2[:]))
             minus_b.append(picked)
@@ -214,14 +234,14 @@ def tile_list_driving_test_assignment_kernel(
             codes, plane = weight
             windows = []
             for i in range(4):
-                window = placed([P, S], F32, "d_win%d%d" % (g, i), [[64, 68, 72, 76], [48, 56, 60, 164]][g][i])
+                window = placed([P, S], F32, "d_win%d%d" % (g, i), [[64, 68, 72, 76], [20, 56, 60, 164]][g][i])
                 cols = slice(P * i, P * (i + 1))
-                first_stage(window, [(codes[:, cols], plane[:, cols], v3, sc3, 12)])
+                first_stage(window, [(codes[:, cols], plane[:, cols], v3, sc3, 0)])
                 windows.append(window)
             return windows
 
         def make_a_slice(g, i, weights):
-            window = placed([P, S], F32, "a_win%d%d" % (g, i), [[32, 36, 40, 44], [0, 4, 8, 12]][g][i])
+            window = placed([P, S], F32, "a_win%d%d" % (g, i), [[32, 36, 40, 44], [128, 132, 136, 140]][g][i])
             cols = slice(P * i, P * (i + 1))
             first_stage(window, [(weights[a][0][:, cols], weights[a][1][:, cols], v1[a], sc1, 4 * a) for a in range(2)])
             return window
@@ -240,7 +260,7 @@ def tile_list_driving_test_assignment_kernel(
 
         def make_dist_bd(g, blocks, picked):
             for i, jb in enumerate(blocks):
-                result = placed([P, KP], F32, "dist_bd%d%d" % (g, jb), 16 + 2 * (4 * g + jb))
+                result = placed([P, KP], F32, "dist_bd%d%d" % (g, jb), 48 + 2 * jb)
                 abs_difference(
                     result,
                     [minus_b[4 * g + s][:, P * jb : P * (jb + 1)] for s in range(4)],
@@ -248,15 +268,12 @@ def tile_list_driving_test_assignment_kernel(
                 )
                 dist_bd[g, jb] = result
 
-        def w1_part(a, g, on_scalar, slot):
-            raw = load_weight(w1[KP * a : KP * (a + 1), BANK * g : BANK * (g + 1)])
-            return quantize_weight(raw, "w1_%d%d" % (a, g), on_scalar, slot, DEALT[g])
 
         z_q = {}
 
         def make_dist_ab(g, jb, picked):
             cols = slice(P * jb, P * (jb + 1))
-            dist_ab = ring.tile([P, KP], F32, name="dist_ab", bufs=3)
+            dist_ab = placed([P, KP], F32, "dist_ab%d%d" % (g, jb), 32 + 2 * jb)
             abs_difference(dist_ab, [minus_b[4 * g + i][:, cols] for i in range(4)], picked)
             return dist_ab
 
@@ -267,9 +284,8 @@ def tile_list_driving_test_assignment_kernel(
                 [(t, dist_ab[:, P * t : P * (t + 1)]) for t in range(PACK)],
                 [(t, dist_bd[g, jb][:, P * t : P * (t + 1)]) for t in range(PACK)],
             )
-            rounded = placed([P, KP], BF16, "z_rounded%d%d" % (g, jb), WORK + 4 * (4 + g) + jb)
-            copy = nc.vector.tensor_copy if jb >= 2 else nc.scalar.copy
-            copy(
+            rounded = placed([P, KP], BF16, "z_rounded%d%d" % (g, jb), WORK + 8 + jb)
+            nc.scalar.copy(
                 rounded[:].rearrange("p (j t) -> p j t", t=PACK),
                 bank[:].rearrange("p (t j) -> p j t", t=PACK),
             )
@@ -328,23 +344,26 @@ def tile_list_driving_test_assignment_kernel(
 
         for s in range(4):
             make_b(s)
-        v3 = gather_words(tab3_win, idx3, "v3")
-        sc3 = gather_scales(sc3_win, idx3, "sc3")
+        v3 = gather_words(tab3_win, idx3, "v3", 116)
         for s in range(4, 8):
             make_b(s)
-        d_win0 = make_d(0, w3_q0)
-        v1.append(gather_words(tab_win[0], idx1, "v1_0"))
-        sc1 = gather_scales(sc1_win, idx1, "sc1")
-        v1.append(gather_words(tab_win[1], idx1, "v1_1"))
-        w3_q1 = quantize_weight(load_weight(w3[:, BANK : 2 * BANK]), "w3_1", True, 0, DEALT[1])
-        w1_q1 = [w1_part(0, 1, True, 1), w1_part(1, 1, True, 5)]
-        w1_q0.append(w1_part(1, 0, True, 4))
-        w5_q = [quantize_weight(load_weight(w5[0:KP, :]), "w5_0", True, 2)]
+        d_win0 = make_d(0, w3_q[0])
+        d_win1 = make_d(1, w3_q[1])
+        v1.append(gather_words(tab_win[0], idx1, "v1_0", 108))
+        v1.append(gather_words(tab_win[1], idx1, "v1_1", 124))
+        w1_q = [[], []]
+        for a in range(2):
+            raw = load_weight(w1[KP * a : KP * (a + 1), :], 144 - 16 * a)
+            for g in range(2):
+                part = raw[:, :, BANK * g : BANK * (g + 1)]
+                w1_q[g].append(quantize_weight(part, "w1_%d%d" % (a, g), True, [[116, WORK + 20], [WORK, WORK + 4]][a][g], DEALT[g]))
+        w1_q0, w1_q1 = w1_q
+        d_picked = pick(d_win0, p3[:], "d_picked0", [0 - WORK, 2 - WORK, 4 - WORK, 6 - WORK])
+        diff_d = [distance(d_win1, p3, 1, 256 * h, 256, "diff_d%d" % h, [8, WORK + 4][h], None) for h in range(2)]
         a_win0 = make_a(0, w1_q0)
-        d_win1 = make_d(1, w3_q1)
-        make_dist_bd(0, range(4), pick(d_win0, p3[:], "d_picked0", [136 - WORK, 138 - WORK, 140 - WORK, 142 - WORK]))
-        picked = pick(a_win0, p1[:], "a_picked0", [8, 10, 12, 14])
-        w5_q.append(quantize_weight(load_weight(w5[KP : 2 * KP, :]), "w5_1", True, 4))
+        w5_q = [quantize_weight(load_weight(w5[0:KP, :], 144)[:], "w5_0", False, WORK + 8)]
+        picked = pick(a_win0, p1[:], "a_picked0", [12, 14, 16, 18])
+        w5_q.append(quantize_weight(load_weight(w5[KP : 2 * KP, :], 152)[:], "w5_1", False, WORK + 20))
         w4_codes = keep.tile([P, 2 * 2 * N], U8, name="w4_codes", align_bytes=64)
         nc.sync.dma_start(
             w4_codes[:].bitcast(I32).rearrange("p (a c) -> p a c", a=2),
@@ -356,8 +375,8 @@ def tile_list_driving_test_assignment_kernel(
                 w4_scales[:, 4 * q : 4 * q + 4, :].bitcast(I32).rearrange("a r c -> r a c"),
             )
 
-        diff_d = distance(d_win1, p3, 1, 0, J, "diff_d", WORK, None)
         a_win1 = make_a(1, w1_q1)
+        make_dist_bd(0, range(4), d_picked)
         dist = [make_dist_ab(0, jb, [x[:, P * jb : P * (jb + 1)] for x in picked]) for jb in range(2)]
         for jb in range(4):
             if jb + 2 < 4:
@@ -366,14 +385,14 @@ def tile_list_driving_test_assignment_kernel(
         banks = [(next_bank("product"), next_bank("product")) for jb in range(4)]
         for jb in range(4):
             second_pass(jb, 0, banks[jb])
-        dist_d = placed([P, 4 * J], F32, "dist_d", 16)
+        dist_d = placed([P, 4 * J], F32, "dist_d", 0)
         for half in range(2):
-            absolute(diff_d, dist_d[:, 1024 * half : 1024 * (half + 1)], 256 * half, 256)
-            diff = distance(a_win1, p1, 1, 256 * half, 256, "diff_a%d" % half, [WORK + 20, 48][half], None)
+            absolute(diff_d[half], dist_d[:, 1024 * half : 1024 * (half + 1)], 0, 256)
+            diff = distance(a_win1, p1, 1, 256 * half, 256, "diff_a%d" % half, [56, WORK + 20][half], None)
             for i in range(2):
                 jb = 2 * half + i
-                dist_a = ring.tile([P, KP], F32, name="dist_ab", bufs=3)
+                dist_a = placed([P, KP], F32, "dist_a%d" % jb, [8, WORK + 4][half] + 2 * i)
                 absolute(diff, dist_a[:], P * i, P)
-                join(1, jb, 1, dist_a[:], dist_d[:, KP * jb : KP * (jb + 1)], WORK + 8 + jb)
+                join(1, jb, 1, dist_a[:], dist_d[:, KP * jb : KP * (jb + 1)], WORK + 12 + jb)
                 second_pass(jb, 1, banks[jb])
                 finish(jb, banks[jb])

@@ -349,8 +349,8 @@ def tile_list_driving_test_assignment_kernel(
             make_b(s)
         d_win0 = make_d(0, w3_q[0])
         d_win1 = make_d(1, w3_q[1])
-        v1.append(gather_words(tab_win[0], idx1, "v1_0", 108))
-        v1.append(gather_words(tab_win[1], idx1, "v1_1", 124))
+        v1.append(gather_words(tab_win[0], idx1, "v1_0", 168))
+        v1.append(gather_words(tab_win[1], idx1, "v1_1", 172))
         w1_q = [[], []]
         for a in range(2):
             raw = load_weight(w1[KP * a : KP * (a + 1), :], 144 - 16 * a)
@@ -385,14 +385,14 @@ def tile_list_driving_test_assignment_kernel(
         banks = [(next_bank("product"), next_bank("product")) for jb in range(4)]
         for jb in range(4):
             second_pass(jb, 0, banks[jb])
-        dist_d = placed([P, 4 * J], F32, "dist_d", 0)
         for half in range(2):
-            absolute(diff_d[half], dist_d[:, 1024 * half : 1024 * (half + 1)], 0, 256)
-            diff = distance(a_win1, p1, 1, 256 * half, 256, "diff_a%d" % half, [56, WORK + 20][half], None)
+            dist_d = placed([P, 4 * 256], F32, "dist_d%d" % half, [4, WORK + 16][half])
+            absolute(diff_d[half], dist_d[:], 0, 256)
+            diff = distance(a_win1, p1, 1, 256 * half, 256, "diff_a%d" % half, [56, 0][half], None)
             for i in range(2):
                 jb = 2 * half + i
-                dist_a = placed([P, KP], F32, "dist_a%d" % jb, [8, WORK + 4][half] + 2 * i)
+                dist_a = placed([P, KP], F32, "dist_a%d" % jb, 32 + 2 * jb)
                 absolute(diff, dist_a[:], P * i, P)
-                join(1, jb, 1, dist_a[:], dist_d[:, KP * jb : KP * (jb + 1)], WORK + 12 + jb)
+                join(1, jb, 1, dist_a[:], dist_d[:, KP * i : KP * (i + 1)], WORK + 12 + jb)
                 second_pass(jb, 1, banks[jb])
                 finish(jb, banks[jb])

from contextlib import ExitStack

import concourse.mybir as mybir
from concourse.masks import make_identity

K, K2, H, N, T, S, J = 1024, 512, 1024, 512, 4096, 1024, 512
FLOPS = 2 * H * S * (K + 2 * K2) + 2 * 2 * H * N * J

F32 = mybir.dt.float32
BF16 = mybir.dt.bfloat16
I32 = mybir.dt.int32
U32 = mybir.dt.uint32
U16 = mybir.dt.uint16
U8 = mybir.dt.uint8
FP8X4 = mybir.dt.float8_e4m3fn_x4
FP4X4 = mybir.dt.float4_e2m1fn_x4
ACT = mybir.ActivationFunctionType
ALU = mybir.AluOpType

P = 128
PACK = 4
KP = P * PACK
BANK = 512
KIB = 1024
B_WINDOWS = 3
BANKS = 8
WORK = 80
DEALT = [False, True]


def tile_list_driving_test_assignment_kernel(
    tc, tab_words, tab_scales, tab2_words, tab2_scales, tab3_words, tab3_scales,
    offs, offs2, offs3, pos1, pos2, pos3,
    w1, w2_words, w2_scales, w3, w4_words, w4_scales, w5, out,
):
    nc = tc.nc
    with ExitStack() as ctx:
        lists = ctx.enter_context(tc.tile_pool(name="lists", bufs=1))
        keep = ctx.enter_context(tc.tile_pool(name="keep", bufs=1))
        arena = ctx.enter_context(tc.tile_pool(name="arena", bufs=1))
        ring = ctx.enter_context(tc.tile_pool(name="ring", bufs=1))
        psum = ctx.enter_context(tc.psum_pool(name="psum", bufs=1))

        banks_taken = []
        last_bank = {}
        ring_of = {"turn": range(BANKS), "product": range(BANKS)}

        def next_bank(kind):
            banks = ring_of[kind]
            n = last_bank.get(banks, -1) + 1
            last_bank[banks] = n
            bank = psum.tile([P, BANK], F32, name="bank%d" % len(banks_taken), offset=banks[n % len(banks)] * 2 * KIB)
            banks_taken.append(bank)
            return bank

        raws = []

        def load_list(source, name):
            tile = lists.tile(list(source.shape), U16, name=name)
            nc.sync.dma_start(tile[:], source)
            return tile

        def placed(shape, dtype, name, kib):
            return arena.tile(shape, dtype, name=name, offset=kib * KIB, align_bytes=64)

        def zeroed_plane(tile):
            nc.vector.memset(tile[:].bitcast(I32), 0)
            return tile

        def load_plane(plane, scales):
            for q in range(4):
                nc.sync.dma_start(plane[32 * q : 32 * q + 4, :].bitcast(I32), scales[0, 4 * q : 4 * q + 4, :].bitcast(I32))

        def load_spread(window, scales):
            passes = scales.shape[0]
            source = scales.bitcast(I32).rearrange("a i t -> i a t") if passes > 1 else scales[0].bitcast(I32)
            nc.sync.dma_start(window[0 : P : 8 // passes, :].bitcast(I32), source)

        def gather_plane(window, offsets, passes, plane, name):
            picked = gather_scales(window, offsets, name)
            for a in range(passes):
                for q in range(4):
                    first = 32 * q + 4 * a
                    nc.gpsimd.dma_start(
                        plane[first : first + 4, :].bitcast(I32), picked[first : 32 * (q + 1) : 8, :].bitcast(I32)
                    )
            return plane

        def load_words(tile, words):
            nc.sync.dma_start(tile[:], words.rearrange("p t i -> p (t i)").bitcast(I32))

        def gather_scales(window, offsets, name):
            picked = keep.tile([P, S], U8, name=name, align_bytes=64)
            nc.vector.tensor_copy(picked[:], window[:].indirect(offsets[:]))
            return picked

        def gather_words(window, offsets, name, place):
            halves = []
            for h in range(2):
                picked = placed([P, BANK], U32, "%s_%d" % (name, h), place + 2 * h)
                nc.vector.tensor_copy(picked[:], window[:].bitcast(U32).indirect(offsets[:, 32 * h : 32 * (h + 1)]))
                halves.append(picked)
            return halves

        def load_weight(rows, kib):
            raw = placed([P, PACK, rows.shape[1]], F32, "raw%d" % len(raws), kib)
            raws.append(raw)
            nc.sync.dma_start(raw[:], rows.rearrange("(p t) c -> p t c", t=PACK))
            return raw

        def quantize_weight(raw, name, on_scalar, place, dealt=False, kept=None):
            rounded = placed([P, PACK * BANK], BF16, name + "_rounded", place)
            dst = rounded[:].rearrange("p (c i t) -> p c t i", i=4, t=PACK)
            src = raw.rearrange("p t (c i) -> p c t i", i=4)
            if dealt:
                dst = rounded[:].rearrange("p (u m t) -> p m u t", u=PACK, t=PACK)
                src = raw.rearrange("p t (m u) -> p m u t", u=PACK)
            if on_scalar:
                nc.scalar.copy(dst, src)
            else:
                nc.vector.tensor_copy(dst, src)
            if kept is None:
                codes = keep.tile([P, BANK], U32, name=name + "_codes", align_bytes=64)
                plane = keep.tile([P, BANK], U8, name=name + "_plane", align_bytes=64)
            else:
                codes = placed([P, BANK], U32, name + "_codes", kept[0])
                plane = placed([P, BANK], U8, name + "_plane", kept[1])
            nc.vector.quantize_mx(out=codes[:].bitcast(FP8X4), scales=plane[:], in_=rounded[:])
            return codes, plane

        def first_stage(window, passes):
            for h in range(2):
                bank = next_bank("product")
                for i, (codes, plane, halves, picked_plane, row) in enumerate(passes):
                    nc.tensor.matmul_mx(
                        out=bank[:], lhsT=codes.bitcast(FP8X4), lhsT_scale=plane,
                        rhs=halves[h][:].bitcast(FP8X4),
                        rhs_scale=picked_plane[row:P, BANK * h : BANK * (h + 1)],
                        start=(i == 0), stop=(i == len(passes) - 1),
                    )
                nc.scalar.copy(window[:, BANK * h : BANK * (h + 1)], bank[:])

        def add_transposed(bank, first, second):
            terms = first + second
            for i, (c, x) in enumerate(terms):
                nc.tensor.matmul(
                    bank[:, P * c : P * (c + 1)], lhsT=x, rhs=ident[:],
                    start=(i == 0), stop=(i == len(terms) - 1), is_transpose=True,
                )

        def abs_difference(result, minus_b, picked):
            bank = next_bank("turn")
            add_transposed(bank, list(enumerate(picked))[::-1], list(enumerate(minus_b)))
            nc.scalar.activation(
                out=result[:].rearrange("j (t m) -> j t m", t=PACK),
                in_=bank[:].rearrange("j (m t) -> j t m", t=PACK), func=ACT.Abs,
            )

        def w2_part(g):
            cols = slice(KP * g, KP * (g + 1))
            if not DEALT[g]:
                return w2_codes[:, cols], w2_plane[:, cols]
            codes = keep.tile([P, KP], I32, name="w2_dealt_codes%d" % g, align_bytes=64)
            plane = keep.tile([P, KP], U8, name="w2_dealt_plane%d" % g, align_bytes=64)
            for dst, src in ((codes, w2_codes), (plane, w2_plane)):
                nc.vector.tensor_copy(
                    dst[:].rearrange("p (u m) -> p m u", u=PACK), src[:, cols].rearrange("p (m u) -> p m u", u=PACK)
                )
            return codes[:], plane[:]

        sc2_win = zeroed_plane(placed([P, T], U8, "sc2_win", 48))
        sc3_win = placed([P, T], U8, "sc3_win", 52)
        nc.gpsimd.memset(sc3_win[:].bitcast(I32), 0)
        sc1_win = zeroed_plane(placed([P, T], U8, "sc1_win", 56))
        w2_plane = zeroed_plane(keep.tile([P, H], U8, name="w2_plane", align_bytes=64))
        w4_plane = zeroed_plane(keep.tile([P, 2 * N], U8, name="w4_plane", align_bytes=64))
        planes = [zeroed_plane(placed([P, S], U8, "plane%d" % i, kib)) for i, kib in enumerate((180, WORK, 181))]
        b_win = [placed([P, 2 * S], F32, "b_win%d" % i, 104 + 8 * i) for i in range(B_WINDOWS)]
        ident = keep.tile([P, P], F32, name="ident")
        for window in b_win:
            nc.vector.memset(window[:, S:], 0.0)
        make_identity(nc, ident[:])

        idx2 = load_list(offs2, "idx2")
        idx3 = load_list(offs3, "idx3")
        idx1 = load_list(offs, "idx1")
        w3_raw = [load_weight(w3[:, 0:BANK], 128)]
        p2 = load_list(pos2, "p2")
        p3 = load_list(pos3, "p3")
        p1 = load_list(pos1, "p1")
        load_spread(sc2_win, tab2_scales)
        load_spread(sc3_win, tab3_scales)
        load_spread(sc1_win, tab_scales)
        w3_raw.append(load_weight(w3[:, BANK : 2 * BANK], 136))
        tab2_win = placed([P, T], I32, "tab2_win", 184)
        load_words(tab2_win, tab2_words[0])
        w2_codes = keep.tile([P, H], I32, name="w2_codes", align_bytes=64)
        load_words(w2_codes, w2_words[0])
        load_plane(w2_plane, w2_scales)
        tab3_win = placed([P, T], I32, "tab3_win", 16)
        load_words(tab3_win, tab3_words[0])
        tab_win = [placed([P, T], I32, "tab_win0", 32), placed([P, T], I32, "tab_win1", 0)]
        load_words(tab_win[0], tab_words[0])

        sc2 = gather_plane(sc2_win, idx2, 1, planes[0], "sc2")
        sc3 = gather_plane(sc3_win, idx3, 1, planes[1], "sc3")
        w3_q = [quantize_weight(w3_raw[0][:], "w3_0", True, WORK + 8, DEALT[0])]
        sc1 = gather_plane(sc1_win, idx1, 2, planes[2], "sc1")
        w3_q.append(quantize_weight(w3_raw[1][:], "w3_1", True, WORK + 12, DEALT[1], (WORK + 4, WORK + 20)))
        v2 = gather_words(tab2_win, idx2, "v2", 176)
        w2_q = [w2_part(0), w2_part(1)]
        load_words(tab_win[1], tab_words[1])

        minus_b = []

        def make_b(s):
            cols = slice(P * (s % 4), P * (s % 4 + 1))
            picked = placed([P, J], F32, "b_picked%d" % s, [160, 162, 16, 18, 24, 26, 28, 30][s])
            passes = [(w2_q[s // 4][0][:, cols], w2_q[s // 4][1][:, cols], v2, sc2, 0)]
            if s < 4:
                window = b_win[s % B_WINDOWS]
                first_stage(window, passes)
                nc.vector.tensor_scalar(picked[:], window[:].indirect(p2[:]), -1.0, 0.0, ALU.mult, ALU.add)
            else:
                window = placed([P, S], F32, "b_win%d" % s, [48, 52, 168, 172][s - 4])
                first_stage(window, passes)
                nc.vector.tensor_copy(picked[:], window[:].indirect(p2[:]))
            minus_b.append(picked)

        dist_bd = {}
        v1 = []

        def make_d(g, weight):
            codes, plane = weight
            windows = []
            for i in range(4):
                window = placed([P, S], F32, "d_win%d%d" % (g, i), [[64, 68, 72, 76], [20, 56, 60, 164]][g][i])
                cols = slice(P * i, P * (i + 1))
                first_stage(window, [(codes[:, cols], plane[:, cols], v3, sc3, 0)])
                windows.append(window)
            return windows

        def make_a_slice(g, i, weights):
            window = placed([P, S], F32, "a_win%d%d" % (g, i), [[32, 36, 40, 44], [128, 132, 136, 140]][g][i])
            cols = slice(P * i, P * (i + 1))
            first_stage(window, [(weights[a][0][:, cols], weights[a][1][:, cols], v1[a], sc1, 4 * a) for a in range(2)])
            return window

        def make_a(g, weights):
            return [make_a_slice(g, i, weights) for i in range(4)]

        def pick(windows, offsets, name, places):
            picked = []
            entries = 16 * offsets.shape[1]
            for i, window in enumerate(windows):
                tile = placed([P, entries], F32, "%s%d" % (name, i), WORK + places[i])
                nc.vector.tensor_copy(tile[:], window[:].indirect(offsets))
                picked.append(tile)
            return picked

        def make_dist_bd(g, blocks, picked):
            for i, jb in enumerate(blocks):
                result = placed([P, KP], F32, "dist_bd%d%d" % (g, jb), 48 + 2 * jb)
                abs_difference(
                    result,
                    [minus_b[4 * g + s][:, P * jb : P * (jb + 1)] for s in range(4)],
                    [x[:, P * i : P * (i + 1)] for x in picked],
                )
                dist_bd[g, jb] = result


        z_q = {}

        def make_dist_ab(g, jb, picked):
            cols = slice(P * jb, P * (jb + 1))
            dist_ab = placed([P, KP], F32, "dist_ab%d%d" % (g, jb), 32 + 2 * jb)
            abs_difference(dist_ab, [minus_b[4 * g + i][:, cols] for i in range(4)], picked)
            return dist_ab

        def make_z(g, jb, dist_ab):
            bank = next_bank("turn")
            add_transposed(
                bank,
                [(t, dist_ab[:, P * t : P * (t + 1)]) for t in range(PACK)],
                [(t, dist_bd[g, jb][:, P * t : P * (t + 1)]) for t in range(PACK)],
            )
            rounded = placed([P, KP], BF16, "z_rounded%d%d" % (g, jb), WORK + 8 + jb)
            nc.scalar.copy(
                rounded[:].rearrange("p (j t) -> p j t", t=PACK),
                bank[:].rearrange("p (t j) -> p j t", t=PACK),
            )
            codes = keep.tile([P, P], U32, name="z_codes%d%d" % (g, jb), align_bytes=64)
            plane = keep.tile([P, P], U8, name="z_plane%d%d" % (g, jb), align_bytes=64)
            nc.vector.quantize_mx(out=codes[:].bitcast(FP8X4), scales=plane[:], in_=rounded[:])
            z_q[g, jb] = (codes[:], plane[:])

        def second_pass(jb, g, banks):
            for bank, codes, plane, width, dtype in (
                (banks[0], w4_codes[:, 2 * N * g : 2 * N * (g + 1)], w4_plane[:, N * g : N * (g + 1)], 2 * P, FP4X4),
                (banks[1], w5_q[g][0][:], w5_q[g][1][:], P, FP8X4),
            ):
                for nb in range(4):
                    nc.tensor.matmul_mx(
                        out=bank[:, P * nb : P * (nb + 1)],
                        lhsT=codes[:, width * nb : width * (nb + 1)].bitcast(dtype),
                        lhsT_scale=plane[:, P * nb : P * (nb + 1)],
                        rhs=z_q[g, jb][0].bitcast(FP8X4), rhs_scale=z_q[g, jb][1],
                        start=(g == 0 and nb == 0), stop=(g == 1 and nb == 3),
                    )

        def finish(jb, banks):
            gate = placed([P, BANK], F32, "gate%d" % jb, 64 + 4 * jb)
            nc.scalar.activation(out=gate[:], in_=banks[0][:], func=ACT.Sigmoid)
            result = placed([P, BANK], F32, "result%d" % jb, 66 + 4 * jb)
            nc.vector.tensor_tensor(result[:], banks[1][:], gate[:], ALU.add)
            nc.sync.dma_start(
                out.rearrange("(nb p) j -> p nb j", p=P)[:, :, P * jb : P * (jb + 1)],
                result[:].rearrange("p (nb j) -> p nb j", nb=4),
            )

        def distance(windows, offsets, g, first, count, name, place, result):
            diff = placed([P, PACK, count], F32, name, place)
            for u in range(PACK):
                nc.vector.tensor_tensor(
                    diff[:, u, :], windows[u][:].indirect(offsets[:, first // 16 : (first + count) // 16]),
                    minus_b[4 * g + u][:, first : first + count], ALU.subtract,
                )
            return diff

        def absolute(diff, result, first, count):
            nc.scalar.activation(
                out=result.rearrange("p (c i u) -> p c u i", i=4, u=PACK),
                in_=diff[:, :, first : first + count].rearrange("p u (c i) -> p c u i", i=4), func=ACT.Abs,
            )

        def join(g, jb0, blocks, x, y, place):
            rounded = placed([P, KP * blocks], BF16, "z_rounded%d%d" % (g, jb0), place)
            nc.vector.tensor_tensor(rounded[:], x, y, ALU.add)
            codes = keep.tile([P, P * blocks], U32, name="z_codes%d%d" % (g, jb0), align_bytes=64)
            plane = keep.tile([P, P * blocks], U8, name="z_plane%d%d" % (g, jb0), align_bytes=64)
            nc.vector.quantize_mx(out=codes[:].bitcast(FP8X4), scales=plane[:], in_=rounded[:])
            for i in range(blocks):
                z_q[g, jb0 + i] = (codes[:, P * i : P * (i + 1)], plane[:, P * i : P * (i + 1)])

        for s in range(4):
            make_b(s)
        v3 = gather_words(tab3_win, idx3, "v3", 116)
        for s in range(4, 8):
            make_b(s)
        d_win0 = make_d(0, w3_q[0])
        d_win1 = make_d(1, w3_q[1])
        v1.append(gather_words(tab_win[0], idx1, "v1_0", 168))
        v1.append(gather_words(tab_win[1], idx1, "v1_1", 172))
        w1_q = [[], []]
        for a in range(2):
            raw = load_weight(w1[KP * a : KP * (a + 1), :], 144 - 16 * a)
            for g in range(2):
                part = raw[:, :, BANK * g : BANK * (g + 1)]
                w1_q[g].append(quantize_weight(part, "w1_%d%d" % (a, g), True, [[116, WORK + 20], [WORK, WORK + 4]][a][g], DEALT[g]))
        w1_q0, w1_q1 = w1_q
        d_picked = pick(d_win0, p3[:], "d_picked0", [0 - WORK, 2 - WORK, 4 - WORK, 6 - WORK])
        diff_d = [distance(d_win1, p3, 1, 256 * h, 256, "diff_d%d" % h, [8, WORK + 4][h], None) for h in range(2)]
        a_win0 = make_a(0, w1_q0)
        w5_q = [quantize_weight(load_weight(w5[0:KP, :], 144)[:], "w5_0", False, WORK + 8)]
        picked = pick(a_win0, p1[:], "a_picked0", [12, 14, 16, 18])
        w5_q.append(quantize_weight(load_weight(w5[KP : 2 * KP, :], 152)[:], "w5_1", False, WORK + 20))
        w4_codes = keep.tile([P, 2 * 2 * N], U8, name="w4_codes", align_bytes=64)
        nc.sync.dma_start(
            w4_codes[:].bitcast(I32).rearrange("p (a c) -> p a c", a=2),
            w4_words.bitcast(I32).rearrange("a p c -> p a c"),
        )
        for q in range(4):
            nc.sync.dma_start(
                w4_plane[32 * q : 32 * q + 4, :].bitcast(I32).rearrange("r (a c) -> r a c", a=2),
                w4_scales[:, 4 * q : 4 * q + 4, :].bitcast(I32).rearrange("a r c -> r a c"),
            )

        a_win1 = make_a(1, w1_q1)
        make_dist_bd(0, range(4), d_picked)
        dist = [make_dist_ab(0, jb, [x[:, P * jb : P * (jb + 1)] for x in picked]) for jb in range(2)]
        for jb in range(4):
            if jb + 2 < 4:
                dist.append(make_dist_ab(0, jb + 2, [x[:, P * (jb + 2) : P * (jb + 3)] for x in picked]))
            make_z(0, jb, dist[jb])
        banks = [(next_bank("product"), next_bank("product")) for jb in range(4)]
        for jb in range(4):
            second_pass(jb, 0, banks[jb])
        for half in range(2):
            dist_d = placed([P, 4 * 256], F32, "dist_d%d" % half, [4, WORK + 16][half])
            absolute(diff_d[half], dist_d[:], 0, 256)
            diff = distance(a_win1, p1, 1, 256 * half, 256, "diff_a%d" % half, [56, 0][half], None)
            for i in range(2):
                jb = 2 * half + i
                dist_a = placed([P, KP], F32, "dist_a%d" % jb, 32 + 2 * jb)
                absolute(diff, dist_a[:], P * i, P)
                join(1, jb, 1, dist_a[:], dist_d[:, KP * i : KP * (i + 1)], WORK + 12 + jb)
                second_pass(jb, 1, banks[jb])
                finish(jb, banks[jb])
